import numpy as np, ml_dtypes
CORES = [83,85,87,115,117,119]
N = 6
BF = ml_dtypes.bfloat16
def gentries(a):
    return np.ascontiguousarray(a.reshape(8, 16, -1).transpose(0, 2, 1)).reshape(8, -1)
def gtable(e):
    e = np.asarray(e); return np.ascontiguousarray(e.reshape(8, -1, 16).transpose(0, 2, 1)).reshape(128, -1).astype(np.int32)
W, TT, M, Q, SC = 2048, 2, 3, 2, 0.5
def tries(prev, cur, c):
    cs, ds = [], []
    for m in range(M):
        v = np.take_along_axis(prev, c[:, None, :], 2) - cur; d = np.add.reduce(v * v, axis=1)
        cs.append(c); ds.append(d); c = (5 * c + d + 1) & (W - 1)
    return np.stack(cs, axis=1), np.stack(ds, axis=1)
def parts(rng):
    return rng.integers(0, 16, (N, 8, 16, TT, W)), rng.integers(0, 16, (N, 8, 16, W)), rng.integers(0, 256, (N, 8, 16, W)), rng.integers(0, W, (N, 8, TT, W))
def walk(x, xb, c):
    d = np.zeros((N, 8, M, TT, W), np.int64); prev = xb[0]
    for r in range(N):
        for s in range(TT):
            cur = x[r, :, :, s]; d[r, :, :, s] = tries(prev, cur, c[r, :, s])[1]; prev = cur
    return d
def pack(x, xb, tb, c, th):
    return {"x": np.ascontiguousarray(x.reshape(N, 128, TT * W)).astype(np.float32).astype(BF), "xb": np.ascontiguousarray(xb.reshape(N, 128, W)).astype(np.float32).astype(BF),
            "tb": np.ascontiguousarray(tb.reshape(N, 128, W)).astype(np.float32).astype(BF),
            "c0": np.stack([gtable(a.reshape(8, -1)) for a in c]), "th": np.stack([gtable(a.reshape(8, -1)) for a in th])}
def setup_inputs(rng):
    x, xb, tb, c = parts(rng)
    th = rng.integers(350, 950, (N, 8, M, TT, W)) + rng.integers(-100, 101, (N, 8, 1, TT, 1))
    return pack(x, xb, tb, c, th)
def setup_inputs_ties(rng):
    x, xb, tb, c = parts(rng); d = walk(x, xb, c)
    return pack(x, xb, tb, c, np.clip(d + rng.integers(-1, 3, d.shape), 0, 4095))
def setup_inputs_counts(rng):
    x, xb, tb, c = parts(rng); d = walk(x, xb, c); a = rng.integers(0, 40, d.shape)
    p = rng.random(d.shape) < rng.random((N, 8, 1, TT, W))
    p[:, 0] = False; p[:, 1] = True; p[:, 2] = False; p[:, 2, M - 1] = True; p[:, 3] = False; p[:, 3, 0] = True
    return pack(x, xb, tb, c, np.where(p, np.minimum(d + 1 + a, 4095), np.maximum(d - a, 0)))
def setup_inputs_ends(rng):
    x, xb, tb, c = parts(rng); x = 15 * (x >> 3); xb = 15 * (xb >> 3); tb = 255 * (tb >> 7)
    even = ((np.arange(N * TT) & 1) == 0).reshape(N, 1, TT, 1)
    x[:, 5] = 15 * even; xb[:, 5] = 0; x[:, 6] = 0; xb[:, 6] = 0
    x[:, 3] = 15; xb[:, 3] = 15; tb[:, 3] = 255
    x[:, 2] = rng.integers(13, 16, (N, 16, TT, W)); xb[:, 2] = rng.integers(13, 16, (N, 16, W)); tb[:, 2] = rng.integers(240, 256, (N, 16, W))
    c = rng.choice(np.array([0, 1, W // 2, W - 1]), (N, 8, TT, W)); c[:, 4] = W - 1; c[:, 7] = 0; c[:, 2] = rng.integers(0, W, (N, TT, W))
    th = 225 * rng.integers(4, 13, (N, 8, M, TT, W)) + rng.integers(0, 2, (N, 8, M, TT, W))
    th[:, 5] = 3600 + rng.integers(0, 2, (N, M, TT, W)); th[:, 6] = rng.integers(0, 2, (N, M, TT, W)); th[:, 0, :, :, ::5] = 4095; th[:, 1, :, :, ::5] = 0
    th[:, 3] = rng.integers(0, 2, (N, M, TT, W)); th[:, 2] = rng.integers(10, 35, (N, M, TT, W))
    return pack(x, xb, tb, c, th)
def setup_inputs_alike(rng):
    x, xb, tb, c = parts(rng)
    x[:, ::2] = np.take_along_axis(rng.integers(0, 16, (N, 4, 16, TT, 8)), rng.integers(0, 8, (N, 4, 1, TT, W)), 4)
    c[:, 1] = rng.integers(0, W, (N, TT, 1)); c[:, 4] = rng.integers(0, W, (N, TT, 1))
    v = rng.integers(0, 15, 16); e = np.zeros(16, np.int64); e[rng.permutation(16)[:3]] = 1
    odd = (np.arange(N * TT) & 1).reshape(N, 1, TT, 1)
    x[:, 3] = v[None, :, None, None] + odd * e[None, :, None, None]; xb[:, 3] = (v + e)[None, :, None]
    same = (W // 8) * rng.integers(1, 9, (N, TT, W)) - 1
    c[:, 3] = np.where(rng.random((N, TT, W)) < 0.8, same, c[:, 3])
    d = walk(x, xb, c); th = np.clip(d + rng.integers(-60, 61, d.shape), 0, 4095)
    th[:, 3] = rng.integers(2, 6, (N, M, TT, W))
    return pack(x, xb, tb, c, th)
def setup_inputs_spread(rng):
    x, xb, tb, c = parts(rng)
    x = (np.exp2(rng.integers(0, 5, (N, 8, 1, TT, W))) * rng.random(x.shape)).astype(np.int64) * (rng.random((N, 8, 1, TT, W)) > 0.0625)
    xb = (np.exp2(rng.integers(0, 5, (N, 8, 1, W))) * rng.random(xb.shape)).astype(np.int64) * (rng.random((N, 8, 1, W)) > 0.0625)
    tb = np.minimum((np.exp2(8 * rng.random((N, 8, 1, W))) * rng.random(tb.shape)).astype(np.int64), 255)
    th = np.clip(np.exp2(12 * rng.random((N, 8, M, TT, W))).astype(np.int64) - 1, 0, 4095)
    return pack(x, xb, tb, c, th)
def check_inputs(d):
    bad = []
    for k, hi in (("x", 15), ("xb", 15), ("tb", 255), ("c0", W - 1), ("th", 4095)):
        v = np.asarray(d[k]).astype(np.float64)
        if np.min(v) < 0 or np.max(v) > hi: bad.append("range of " + k)
        if np.any(v != np.floor(v)): bad.append("whole numbers in " + k)
    return bad
def reference(x, xb, tb, c0, th):
    X = x.astype(np.float32).astype(np.int64).reshape(N, 8, 16, TT, W)
    prev = xb[0].astype(np.float32).astype(np.int64).reshape(8, 16, W); tau = tb[0].astype(np.float64).reshape(8, 16, W)
    C = np.stack([gentries(a) for a in c0]).astype(np.int64).reshape(N, 8, TT, W); H = np.stack([gentries(a) for a in th]).astype(np.int64).reshape(N, 8, M, TT, W)
    J = np.zeros((N, 8, Q, TT, W), np.int64); Y = []
    for r in range(N):
        for s in range(TT):
            cur = X[r, :, :, s]; cs, ds = tries(prev, cur, C[r, :, s])
            ok = ds < H[r, :, :, s]; n = np.add.accumulate(ok.astype(np.int64), axis=1)
            tot = np.zeros((8, 16, W))
            for q in range(Q):
                hit = ok & (n == q + 1)
                j = np.where(np.any(hit, axis=1), np.add.reduce(np.where(hit, cs, 0), axis=1), cs[:, M - 1])
                J[r, :, q, s] = j; tot = tot + np.take_along_axis(tau, j[:, None, :], 2)
            tau = tot * SC + cur; prev = cur
        Y.append(tau.reshape(128, W))
    return {"yj": np.stack([gtable(a.reshape(8, -1)) for a in J]).astype(np.float32), "ytau": np.stack(Y).astype(np.float32)}

from concourse.bass import DstId, RemoteDMATransfer
from concourse.mybir import AluOpType as ALU, ActivationFunctionType as AF

W = 2048
CHAIN = [2, 3, 4, 5]
CONV = {4: (0, 2), 6: (0, 3), 8: (0, 4), 10: (0, 5), 5: (1, 2), 7: (1, 3), 9: (1, 4), 11: (1, 5)}
NSC = {0: [30, 32, 20, 30, 32, 30, 32, 26], 1: [18, 16, 28, 24, 28, 14, 28, 14], 2: [18, 12, 22, 14, 20, 16, 14, 18]}
SEQ = [(0, 0), (1, 0), (0, 1), (2, 0), (1, 1), (3, 0), (2, 1), (3, 1)]
SEQ0 = [(0, 0), (1, 0), (0, 1), (1, 1), (2, 0), (3, 0), (2, 1), (3, 1)]
F1, F0 = 32768, 65536
STEP = ("v:a0 s:g2 s:g1 v:x s:g3 v:b0 p:p30 s:c2b0 s:c2a0 s:c30 p:p10 s:c10 v:a1 v:a2 v:a3 v:b1 s:c2b1 v:b2 s:c2a2 v:b3 v:c2a1 s:c2b3 "
        "p:p11 s:c3b1 s:c11 v:c2b2 v:c2a3 s:c3a1 p:p12 v:c3b2 v:c12 v:c3a2 p:p33 s:c33 p:p13 v:c13").split()
STEP_O = ("v:a0 v:x v:b0 p:p10 p:p30 s:g1 v:a1 s:g2 v:a2 v:b1 s:g3 v:a3 s:c2a0 v:b2 v:b3 s:c2b0 s:o0 s:c2a1 v:c2a2 p:p11 v:c3b1 v:c2a3 "
          "s:c10 p:p12 v:c3b2 v:c12 v:c3a2 p:p13 v:c13 s:c30 s:c2b2 v:o1 s:c2b3 s:c2b1 s:c11 s:c3a1 p:p33 s:c33").split()
STEP_LAST = "v:a0 s:g1 s:g2 s:g3 v:b0 v:a1 v:a2 v:b1 v:a3 s:e0 s:e1 v:b2 v:b3 s:e2 v:e3".split()
OUT_AT = {2: 1, 4: 3, 6: 5, 8: 7, 9: 9}

SCRATCH = {
    "xp": ("sbuf", [128, W], "bfloat16"), "xs": ("sbuf", [128, 2, W], "bfloat16"),
    "res": ("sbuf", [128, 6, 5, 128], "int32"),
    "u0": ("sbuf", [128, 2, 128], "uint16"), "u1": ("sbuf", [128, 4, 64], "uint16"), "c1t": ("sbuf", [128, 4, 64], "int32"),
    "c50": ("sbuf", [128, 2, 128], "float32"), "c5r": ("sbuf", [128, 2, 128], "float32"),
    "c0k": ("sbuf", [128, 2, 128], "float32"), "c1k": ("sbuf", [128, 2, 128], "int32"), "c1r": ("sbuf", [128, 2, 128], "float32"),
    "k0": ("sbuf", [128, 2, 128], "float32"), "k1": ("sbuf", [128, 2, 128], "float32"), "qq": ("sbuf", [128, 2, 128], "float32"),
    "jk": ("sbuf", [128, 2, 2, 128], "int32"), "ji": ("sbuf", [128, 6, 2, 128], "int32"), "jr": ("sbuf", [128, 2, 2, 128], "float32"),
    "jt": ("sbuf", [128, 2, 256], "float32"), "jy": ("sbuf", [128, 2, 256], "int32"), "jz": ("sbuf", [128, 2, 256], "int32"),
    "jo": ("sbuf", [128, 6, 4, 2, 32], "uint16"), "jf": ("sbuf", [128, 6, 2, 128], "float32"),
    "dif": ("sbuf", [128, 8, 1024], "bfloat16"), "sq": ("sbuf", [128, 8, 1024], "bfloat16"),
    "ones": ("sbuf", [128, 256], "float32"), "rot": ("sbuf", [128, 256], "float32"),
    "t8a": ("sbuf", [128, 8], "float32"), "t8b": ("sbuf", [128, 8], "float32"),
    "wd": ("sbuf", [128, 144], "bfloat16"), "idp": ("sbuf", [128, 128], "bfloat16"), "idn": ("sbuf", [128, 128], "bfloat16"),
    "ids": ("sbuf", [128, 12, 128], "bfloat16"),
    "w0": ("sbuf", [128, W], "float32"), "w1": ("sbuf", [128, W], "float32"),
    "acc": ("sbuf", [128, 2, 512], "float32"), "xl": ("sbuf", [128, 16 * 512], "bfloat16"),
    "ju": ("sbuf", [128, 12, 64], "uint16"), "ob": ("sbuf", [128, 6, 512], "float32"),
    "dx": ("dram", [4, 128, 1024], "bfloat16"), "dtb": ("dram", [4, 128, 512], "bfloat16"),
    "dout": ("dram", [4, 128, 512], "float32"), "dh0": ("dram", [4, 128, 256], "float32"), "dh1": ("dram", [4, 128, 256], "float32"),
}
for _b in range(8):
    SCRATCH["pb%d" % _b] = ("psum", [128, 512], "float32")

SEMAPHORES = (["cv", "cs", "cp", "cgq", "sent", "sxp", "lc0", "lth", "lx00", "lx01", "lx10", "lx11", "lxp", "rmx", "rmt", "lxl", "lwb",
               "fin", "xpa", "tba", "hla", "hlb", "jfa"] + ["ra%d" % i for i in range(2, 6)]
              + ["xa%d" % r for r in range(6)] + ["ja%d" % t for t in range(12)] + ["oa%d" % k for k in range(4)]
              + ["h%d%d" % (h, k) for h in range(2) for k in range(4)])

CY = 1.04
GC = 1.56
PC = 0.5
HOP = 120.0
COUNTER = {"v": "cv", "s": "cs", "p": "cp", "g": "cgq"}
SIZE = {"xp": 524288, "ra": 327680, "jf": 131072, "tb": 131072, "h0": 131072, "h1": 131072}
PLANS = {}


def build_ops():
    ops, lastw, readers = [], {}, {}

    def op(engs, cost, fn, r=(), w=(), sem=None, inc=0, lat=0.0, after=(), rem=False):
        i = len(ops)
        deps = {}
        for k in r:
            for d in lastw.get(k, ()):
                deps[d] = True
        for k in w:
            for d in list(lastw.get(k, ())) + readers.get(k, []):
                deps.setdefault(d, False)
        for d in after:
            deps.setdefault(d, False)
        for k in r:
            readers.setdefault(k, []).append(i)
        for k in w:
            lastw[k] = [i]
            readers[k] = []
        c = cost if isinstance(cost, dict) else {e: cost for e in engs}
        ops.append({"i": i, "engs": engs, "cost": c, "fn": fn, "deps": deps, "prio": i,
                    "sem": sem, "inc": inc, "lat": lat, "rem": rem, "w": (list(w) + ["-"])[0]})
        return i

    return ops, op


def schedule(ops):
    free = {e: 0.0 for e in "vspgy"}
    order = {e: [] for e in "vspgy"}
    done, eng = {}, {}
    gq = [o["i"] for o in ops if o["engs"] == "g"]
    users = {o["i"]: [] for o in ops}
    miss = {}
    for o in ops:
        miss[o["i"]] = len(o["deps"])
        for d in o["deps"]:
            users[d].append(o["i"])
    ready = [o for o in ops if not o["deps"] and o["engs"]]

    def finish(i):
        for u in users[i]:
            miss[u] -= 1
            if miss[u] == 0:
                ready.append(ops[u])

    for o in ops:
        if o["engs"] == "":
            done[o["i"]] = o["lat"]
            eng[o["i"]] = ""
            finish(o["i"])
    while ready:
        cand = []
        for o in ready:
            if o["engs"] == "g" and gq[len(order["g"])] != o["i"]:
                continue
            best = None
            for e in o["engs"]:
                st = free[e]
                for d, raw in o["deps"].items():
                    if raw or eng[d] != e or ops[d]["sem"]:
                        st = max(st, done[d] + HOP)
                if best is None or st + o["cost"][e] < best[0] + o["cost"][best[1]]:
                    best = (st, e)
            cand.append((best[0], o["prio"], best[1], o))
        st, pr, e, o = min(cand, key=lambda c: (c[0], c[1]))
        rivals = [c for c in cand if c[2] == e and c[1] < pr and c[0] < st + min(0.7 * o["cost"][e], 350.0)]
        if rivals:
            st, pr, e, o = min(rivals, key=lambda c: c[1])
        free[e] = st + o["cost"][e]
        done[o["i"]] = free[e] + o["lat"]
        eng[o["i"]] = e
        o["start"] = st
        order[e].append(o["i"])
        ready.remove(o)
        finish(o["i"])
    return order, eng, done


def emit(g, T, ops, order, eng):
    Q = {"v": g.vector, "s": g.scalar, "p": g.tensor, "g": g, "y": g.sync}
    total, tok = {}, {}
    for o in ops:
        if o["sem"]:
            total[o["sem"]] = total.get(o["sem"], 0) + o["inc"]
    needed = set()
    for o in ops:
        for d, raw in o["deps"].items():
            if raw or eng[d] != eng[o["i"]]:
                needed.add(d)
    for e in "vspg":
        plain = [i for i in order[e] if not ops[i]["sem"]]
        if plain:
            needed.add(plain[-1])
        n = 0
        for i in plain:
            if i in needed:
                n += 1
                tok[i] = (COUNTER[e], n)
        total[COUNTER[e]] = n
    for o in ops:
        if o["sem"]:
            tok[o["i"]] = (o["sem"], total[o["sem"]])
    for e in "yspvg":
        seen = {}
        for i in order[e]:
            o = ops[i]
            want = {}
            for d, raw in o["deps"].items():
                if raw or eng[d] != e or ops[d]["sem"]:
                    s, n = tok[d]
                    want[s] = max(want.get(s, 0), n)
            for s in sorted(want):
                if seen.get(s, 0) < want[s]:
                    Q[e].wait_ge(T.sem[s], want[s])
                    seen[s] = want[s]
            ins = o["fn"](Q[e], e)
            if o["sem"]:
                if not o["rem"]:
                    ins.then_inc(T.sem[o["sem"]], 16)
            elif i in tok:
                ins.then_inc(T.sem[tok[i][0]], 1)
        if e == "g":
            for s in sorted(total):
                if total[s] > seen.get(s, 0):
                    g.wait_ge(T.sem[s], total[s])


def xo(t):
    return 512 * (11 - t)


def relays(T, topo):
    src = T.cores[0]
    far = [k for k in range(4) if topo.chip(T.cores[CHAIN[k]]) != topo.chip(src)]
    out = {}
    for c in topo.cores_of(src):
        if c not in T.cores and topo.die(c) == topo.die(src) and len(out) < len(far) - 1 and topo.may_write(c, T.cores[CHAIN[far[len(out)]]]):
            out[far[len(out)]] = c
    return out


def relay_program(g, core, k, T, topo):
    dst = T.cores[CHAIN[k]]
    rid, pid, _ = topo.addr(dst)
    n, es = len(topo.engines(T.cores[0], core)), topo.engines(core, dst)
    for hsem, sem, src, c, w in (("hla", "xa0", T.dx, xo(0), 1024), ("hlb", "tba", T.dtb, xo(1), 512)):
        g.wait_ge(T.sem[hsem], n)
        g.remote_dma(T.xl[:, c:c + w], src[k], T.sem[sem], T.sem.sent, pid, rid, topo.mask(core, dst))
    g.wait_ge(T.sem.sent, 2 * len(es))


def plan(core, T, topo, est):
    rank = T.rank_of(core)
    cores = list(T.cores)
    nr = len(cores)
    ops, op = build_ops()
    kme = CHAIN.index(rank) if rank in CHAIN else None
    lister = kme is None
    pb = [T["pb%d" % b] for b in range(8)]

    def vc(n, f=1.0):
        return 30.0 + max(64, n * f) * CY

    def gat(n):
        return 60.0 + n * GC * CY

    def dma(engs, out, in_, r, w, sem, nbytes, after=()):
        return op(engs, 60.0, lambda q, e: q.dma_start(out, in_), r, w, sem, 16, 2000.0 + nbytes / 250.0, after)

    def bits(es):
        m = 0
        for x in es:
            m |= 1 << x
        return m

    def near(r):
        return topo.chip(cores[r]) == topo.chip(core)

    def remote(to, out, in_, sem, r, local="sent", lat=0.0, core_to=None):
        dst = cores[to] if core_to is None else core_to
        rid, pid, _ = topo.addr(dst)
        es = topo.engines(core, dst)
        i = op("g", 400.0, lambda q, e: q.remote_dma(out, in_, T.sem[sem], T.sem[local], pid, rid, bits(es)),
               r, (), local, len(es), lat, rem=True)
        ops[i]["to"] = [(to, sem, SIZE.get(sem[:2], 262144), near(to))]
        return i

    def list_engines(src):
        kinds = {}
        for c in CHAIN:
            kinds.setdefault(tuple(topo.engines(src, cores[c])), []).append(cores[c])
        used, out = [], {}
        for es in sorted(kinds, key=len):
            left = [x for x in es if x not in used]
            ds = kinds[es]
            for j, d in enumerate(ds):
                share = -(-len(left) // (len(ds) - j))
                n = 1
                while 2 * n <= share + (1 if j == 0 and len(ds) > 2 else 0):
                    n *= 2
                out[d], left = left[:n], left[n:]
                used += out[d]
        return out

    def arrive(sem, frm, w, inc=None):
        return op("", {}, None, (), w, sem, len(topo.engines(cores[frm], core)) if inc is None else inc, est.get((rank, sem), 0.0))

    def copy(engs, out, in_, n, r, w, scale=None, vf=1.0, after=()):
        def fn(q, e):
            if e == "s":
                if scale is None:
                    return q.activation(out, in_, AF.Copy)
                return q.activation(out, in_, AF.Copy, scale=scale)
            if scale is None:
                return q.tensor_copy(out, in_)
            return q.tensor_scalar(out, in_, scale, None, ALU.mult)
        return op(engs, {"v": vc(n, vf), "s": vc(n) + 30.0}, fn, r, w, after=after)

    def tt(out, a, b, alu, n, r, w, f=1.0, after=()):
        return op("v", vc(n, f), lambda q, e: q.tensor_tensor(out, a, b, alu), r, w, after=after)

    def ts(out, a, s1, s2, o0, o1, n, r, w, after=()):
        if s2 is None:
            return op("v", vc(n), lambda q, e: q.tensor_scalar(out, a, s1, None, o0), r, w, after=after)
        return op("v", vc(n), lambda q, e: q.tensor_scalar(out, a, s1, s2, o0, o1), r, w, after=after)

    def loadx(q, s, h, nbytes):
        dma(q, T.xs[:, s, 1024 * h:1024 * h + 1024], T.x[:, W * s + 1024 * h:W * s + 1024 * h + 1024], (), ["xs%d%d" % (s, h)], "lx%d%d" % (s, h), nbytes)

    dma("s", T.res[:, 0:2, 2, :], T.c0[:], (), ["c00", "c01"], "lc0", 131072)
    if rank == 0:
        dma("y", T.xp[:], T.xb[:], (), ["xp"], "lxp", 900000)
        loadx("s", 0, 0, 900000)
        loadx("s", 0, 1, 1150000)
        loadx("y", 1, 0, 1400000)
        loadx("y", 1, 1, 1650000)
    elif rank + 1 < nr and not near(rank + 1):
        loadx("y", 1, 0, 600000)
        loadx("s", 1, 1, 600000)
        loadx("y", 0, 0, 1150000)
        loadx("s", 0, 1, 1150000)
    else:
        loadx("y", 0, 0, 900000)
        loadx("s", 0, 1, 900000)
        loadx("y", 1, 0, 900000)
        loadx("s", 1, 1, 1150000)
    if rank:
        arrive("xpa", rank - 1, ["xp"])
    for m in range(2):
        dma("y", T.res[:, 0:2, 3 + m, :], T.th[:, 256 * m:256 * m + 256], (), ["th%d0" % m, "th%d1" % m], "lth", 1900000)
    xk = [["xs00", "xs01"], ["xs10", "xs11"]]

    op("v", vc(256), lambda q, e: q.memset(T.ones[:], 1.0), (), ["ones"])
    op("v", vc(144, 0.5), lambda q, e: q.memset(T.wd[:], 0.0), (), ["wd"])
    op("g", 200.0, lambda q, e: q.affine_select(T.t8a[:], T.ones[:, 0:8], [[-16, 8]], ALU.is_ge, 0.0, 0, 1), ["ones"], ["t8a"])
    op("g", 700.0, lambda q, e: q.affine_select(T.rot[:], T.ones[:], [[0, 2], [-1, 128]], ALU.is_equal, 0.0, 0, 1), ["ones"], ["rot"])
    op("g", 200.0, lambda q, e: q.affine_select(T.t8b[:], T.t8a[:], [[16, 8]], ALU.is_ge, 0.0, 15, -1), ["t8a"], ["t8b"])
    if lister:
        for q in range(4):
            kq = (W - 512 * q) % W
            for j, val in enumerate((kq + F0, kq, W - kq)):
                op("v", vc(32), lambda qu, e, c=128 * j + 32 * q, val=val: qu.memset(pb[7][:, c:c + 32], float(val)), (), ["kt%d%d" % (j, q)])
    kt = [pb[7][:, 128 * j:128 * j + 128] for j in range(3)]
    ktk = [["kt%d%d" % (j, q) for q in range(4)] for j in range(3)]
    copy("v", T.wd[:, 15:143:16], T.t8b[:], 8, ["t8b", "wd"], ["wd"])
    copy("v", T.idp[:], T.rot[:, 0:128], 128, ["rot"], ["idp"])
    copy("v", T.idn[:], T.rot[:, 0:128], 128, ["rot"], ["idn"], scale=-1.0)
    copy("v", T.u0[:], T.res[:, 0:2, 2, :], 256, ["c00", "c01"], ["u0"])
    ts(T.c50[:], T.res[:, 0:2, 2, :], 5.0, 1.0 + F1, ALU.mult, ALU.add, 256, ["c00", "c01"], ["c50"])
    if not lister:
        for t in range(2 * nr):
            copy("v", T.ids[:, t, :], T.idp[:], 128, ["idp"], ["ids%d" % t], scale=float(2 ** (t + 1)), vf=0.5)

    gate = []
    if rank + 1 < nr:
        gate = [remote(rank + 1, T.xp[:], T.xs[:, 1, :], "xpa", xk[1], "sxp", 2500.0)]

    def remap(dst, c, src, key, sem, when, aft):
        for q in range(4):
            dma("y", dst[:, 32 * q:32 * q + 32, c:c + 512], src(512 * q), when, [key + str(q)], sem, 600000, aft)

    if rank == 0:
        remap(T.dx, 512, lambda c: T.tb[:, c:c + 512], "dx1", "rmx", xk[0] + ["xp"], [])
        remap(T.dx, 0, lambda c: T.x[:, c:c + 512], "dx0", "rmx", xk[0] + ["xp"], [])
        remap(T.dtb, 0, lambda c: T.x[:, W + c:W + c + 512], "dtb", "rmt", xk[1], gate)
    else:
        for s in range(2):
            remap(T.dx, 512 - 512 * s, lambda c, s=s: T.x[:, W * s + c:W * s + c + 512], "dx%d" % s, "rmx", xk[0] + xk[1], gate)
    dxk = ["dx%d%d" % (s, q) for s in range(2) for q in range(4)]

    def send_x():
        c = xo(2 * rank + 1)
        for k in range(4):
            if k != kme:
                remote(CHAIN[k], T.xl[:, c:c + 1024], T.dx[k], "xa%d" % rank, dxk)

    def send_first(src, dst, sem, hsem, keys):
        via = relays(T, topo)
        for k in sorted(range(4), key=lambda k: (k not in via, near(CHAIN[k]))):
            if k in via:
                i = remote(CHAIN[k], src[k], src[k], hsem, keys, core_to=via[k])
                ops[i]["to"] = [(CHAIN[k], sem, SIZE.get(sem[:2], 262144), ("via", k))]
            else:
                remote(CHAIN[k], dst, src[k], sem, keys)

    if rank == 0:
        send_first(T.dx, T.xl[:, xo(0):xo(0) + 1024], "xa0", "hla", dxk)
        send_first(T.dtb, T.xl[:, xo(1):xo(1) + 512], "tba", "hlb", ["dtb%d" % q for q in range(4)])

    def chunk(n, j, s, h, m):
        nsc = NSC[min(rank, 2)][n]
        nv, ns = 1024 - 16 * nsc, 16 * nsc
        win, wk = (T.xp[:, 0:W], ["xp"]) if s == 0 else (T.xs[:, 0, 0:W], xk[0])
        ck, tag, c = ["xs%d%d" % (s, h)], "%d%d" % (s, h), slice(64 * h, 64 * h + 64)

        def cur(a, b):
            return T.xs[:, s, 1024 * h + a:1024 * h + b]

        def u(a, b):
            return T.u0[:, s, 64 * h + a:64 * h + b] if m == 0 else T.u1[:, j, a:b]

        ul = ["u0"] if m == 0 else ["u1%d" % j]
        fb, db = n % 2, (2 + n % 2 if lister else (2, 3, 6, 7)[j])
        cuts = [0, 2 * ((64 - nsc) // 4), 64 - nsc]
        for i in range(2):
            op("v", gat(16 * (cuts[i + 1] - cuts[i])), lambda q, e, a=cuts[i], b=cuts[i + 1]: q.tensor_tensor(
                T.dif[:, n, 16 * a:16 * b], win.indirect(u(a, b)), cur(16 * a, 16 * b), ALU.subtract), wk + ul + ck, ["difv%d_%d" % (n, i)])
        op("s", gat(ns), lambda q, e: q.activation(T.dif[:, n, nv:1024], win.indirect(u(64 - nsc, 64)), AF.Copy), wk + ul, ["difs%d" % n])
        op("p", ns * PC, lambda q, e: q.matmul(pb[fb][:, 0:ns], T.idn[:], cur(nv, 1024), True, False), ["idn"] + ck, ["pb%d" % fb])
        op("p", ns * PC, lambda q, e: q.matmul(pb[fb][:, 0:ns], T.idp[:], T.dif[:, n, nv:1024], False, True),
           ["idp", "difs%d" % n], ["pb%d" % fb, "fp%d" % n])
        for i in range(2):
            op("s", vc(16 * (cuts[i + 1] - cuts[i])) + 30, lambda q, e, a=16 * cuts[i], b=16 * cuts[i + 1]: q.activation(
                T.sq[:, n, a:b], T.dif[:, n, a:b], AF.Square), ["difv%d_%d" % (n, i)], ["sqv%d_%d" % (n, i)])
        op("s", vc(ns) + 30, lambda q, e: q.activation(T.sq[:, n, nv:1024], pb[fb][:, 0:ns], AF.Square), ["fp%d" % n], ["sqs%d" % n, "pb%d" % fb])
        for r in range(16):
            op("p", 64 * PC + 10, lambda q, e, r=r: q.matmul(pb[db][:, 0:64], T.wd[:, 15 - r:143 - r], T.sq[:, n, r:1024:16], r == 0, r == 15),
               ["wd", "sqs%d" % n, "sqv%d_0" % n, "sqv%d_1" % n], ["pb%d" % db] + (["d%d" % n] if r == 15 else []))
        d, dk, bk = pb[db][:, 0:64], "d%d" % n, "pb%d" % db
        if m == 0:
            tt(T.res[:, s, 0, c], d, T.c50[:, s, c], ALU.add, 64, [dk, "c50"], ["ei" + tag, bk])
            ts(T.c1t[:, j, :], T.res[:, s, 0, c], W - 1, None, ALU.bitwise_and, None, 64, ["ei" + tag], ["c1t%d" % j])
            copy("v", T.u1[:, j, :], T.c1t[:, j, :], 64, ["c1t%d" % j], ["u1%d" % j])
        else:
            copy("v", T.res[:, s, 1, c], d, 64, [dk], ["d1" + tag, bk])

    made = []

    def parents(t, slot, after=(), halves=False):
        z = len(made) % 2
        vb = 4 + z
        vk, zs, sl = "pb%d" % vb, str(z), str(slot)
        ok0, e2, ok1, mm = [pb[vb][:, 128 * i:128 * i + 128] for i in range(4)]
        ei, d1, c0, th0, th1 = [T.res[:, slot, i, :] for i in range(5)]
        eik = ["ei%s0" % sl, "ei%s1" % sl]

        def two(x):
            return [x + zs + "0", x + zs + "1"]

        if slot < 2:
            c50, c5k = T.c50[:, slot, :], "c50"
        else:
            c50, c5k = T.c5r[:, z, :], "c5r" + zs
            ts(c50, c0, 5.0, 1.0 + F1, ALU.mult, ALU.add, 128, ["c0" + sl], [c5k], after=after)
        tt(mm, c50, th0, ALU.add, 128, [c5k, "th0" + sl], two("mm") + [vk], 2.0, after=after)
        tt(T.c0k[:, z, :], kt[0], c0, ALU.add, 128, ktk[0] + ["c0" + sl], ["c0k" + zs], after=after)
        ts(T.c1k[:, z, :], ei, W - 1 + F1, None, ALU.bitwise_and, None, 128, eik, ["c1k" + zs], after=after)
        tt(ok0, mm, ei, ALU.is_gt, 128, two("mm") + eik, ["ok0" + zs, vk])
        tt(T.c1r[:, z, :], kt[1], T.c1k[:, z, :], ALU.add, 128, ktk[1] + ["c1k" + zs], ["c1r" + zs])
        tt(T.k0[:, z, :], ok0, T.c0k[:, z, :], ALU.mult, 128, ["ok0" + zs, "c0k" + zs], ["k0" + zs, vk])
        ts(e2, T.c1r[:, z, :], 5.0, 1.0 - 5 * F1, ALU.mult, ALU.add, 128, ["c1r" + zs], two("e2") + [vk])
        copy("v", ok1, th1, 128, ["th1" + sl], two("ok1") + [vk], after=after)
        for hs in ([["0"], ["1"]] if halves else [["0", "1"]]):
            a, b = 64 * int(hs[0]), 64 * int(hs[-1]) + 64
            n = b - a

            def ks(x, y=zs):
                return [x + y + h for h in hs]

            def ps(i):
                return pb[vb][:, 128 * i + a:128 * i + b]

            d1h, k1, qq = T.res[:, slot, 1, a:b], T.k1[:, z, a:b], T.qq[:, z, a:b]
            tt(ps(2), ps(2), d1h, ALU.is_gt, n, ks("ok1") + ks("d1", sl), ks("ok1") + [vk])
            tt(ps(1), ps(1), d1h, ALU.add, n, ks("e2") + ks("d1", sl), ks("e2") + [vk])
            tt(k1, ps(2), T.c1r[:, z, a:b], ALU.mult, n, ks("ok1") + ["c1r" + zs], ks("k1") + [vk])
            tt(ps(3), ps(1), k1, ALU.max, n, ks("e2") + ks("k1"), ks("mm") + [vk])
            tt(qq, ps(0), k1, ALU.mult, n, ["ok0" + zs] + ks("k1"), ks("qq") + [vk])
            tt(T.jk[:, z, 0, a:b], ps(3), T.k0[:, z, a:b], ALU.max, n, ks("mm") + ["k0" + zs], ks("jk0") + [vk])
            tt(T.jk[:, z, 1, a:b], ps(1), qq, ALU.max, n, ks("e2") + ks("qq"), ks("jk1") + [vk])
            for p in range(2):
                ts(T.ji[:, slot, p, a:b], T.jk[:, z, p, a:b], W - 1, None, ALU.bitwise_and, None, n, ks("jk%d" % p), ks("ji%d" % p, sl))
            for p in range(2):
                copy("v", T.jr[:, z, p, a:b], T.ji[:, slot, p, a:b], n, ks("ji%d" % p, sl), ks("jr%d" % p))
        for p in range(2):
            op("p", 512 * PC, lambda q, e, p=p: q.matmul(pb[6][:, 128 * p:128 * p + 128], T.jr[:, z, p, :], T.rot[:, 0:128], True, True),
               two("jr%d" % p) + ["rot"], ["pb6", "jp%d" % p])
        op("v", vc(256), lambda q, e: q.transpose(T.jt[:, z, :], pb[6][:, 0:256]), ["jp0", "jp1"], ["jt" + zs, "pb6"])
        for p in range(2):
            last = copy("v", T.jo[:, slot, :, p, :], T.jt[:, z, 128 * p:128 * p + 128], 128, ["jt" + zs], ["jo%d%s" % (p, sl)])
        es = list_engines(core)
        trs = []
        for k in range(4):
            dst = cores[CHAIN[k]]
            rid, pid, _ = topo.addr(dst)
            trs.append(RemoteDMATransfer(dst_ids=[DstId(rid=rid, pnc=pid)], dma_engine_mask=bits(es[dst]),
                                         remote_sem=T.sem["ja%d" % t], src=T.jo[:, slot, k, :, :], dst=T.ju[:, t, :]))
        i = op("g", 500.0, lambda q, e: q.remote_dma_fused(trs, local_sem=T.sem.sent), ["jo0" + sl, "jo1" + sl], (), "sent",
               sum(len(x) for x in es.values()), rem=True)
        ops[i]["to"] = [(c, "ja%d" % t, 30000, near(c)) for c in CHAIN]
        made.append((t, slot))
        return last

    def plain(t, slot, z, aft):
        sl, zs = str(slot), str(z)
        for p in range(2):
            tt(T.jy[:, z, 128 * p:128 * p + 128], kt[2], T.ji[:, slot, p, :], ALU.add, 128,
               ktk[2] + ["ji%d%s%d" % (p, sl, h) for h in range(2)], ["jy%d%s" % (p, zs)], after=aft)
        ts(T.jz[:, z, :], T.jy[:, z, :], W - 1, None, ALU.bitwise_and, None, 256, ["jy0" + zs, "jy1" + zs], ["jz" + zs])
        copy("v", T.jf[:, slot, :, :], T.jz[:, z, :], 256, ["jz" + zs], ["jf" + sl])
        if slot >= 2:
            remote(t // 2, T.jf[:, t % 2, :, :], T.jf[:, slot, :, :], "jfa", ["jf" + sl])

    def send_res(s):
        to, slot = CONV[2 * rank + s]
        remote(to, T.res[:, slot, :, :], T.res[:, s, :, :], "ra%d" % slot,
               ["%s%d%d" % (x, s, h) for x in ("ei", "d1") for h in range(2)] + ["c0%d" % s, "th0%d" % s, "th1%d" % s])

    s0 = 0 if rank == 0 else 1
    tasks = [(s0, 0), (s0, 1), (1 - s0, 0), (1 - s0, 1)]
    for n, (j, m) in enumerate(SEQ0 if rank == 0 else SEQ):
        chunk(n, j, tasks[j][0], tasks[j][1], m)
        if (j, m) == (1, 1):
            if rank == 0:
                parents(0, 0)
            elif rank == 1:
                send_x()
            else:
                send_res(1)
                if rank > 2:
                    send_x()
    if rank == 0:
        last = parents(1, 1, halves=True)
    elif rank == 1:
        parents(2, 0)
        last = parents(3, 1)
    else:
        send_res(0)
        if rank == 2:
            send_x()
        arrive("jfa", CONV[2 * rank][0], ["jf0"])
        arrive("jfa", CONV[2 * rank + 1][0], ["jf1"])
    if lister:
        gate2 = last
        for t in sorted(CONV):
            to, slot = CONV[t]
            if to == rank:
                sl = str(slot)
                arrive("ra%d" % slot, t // 2, ["ei%s0" % sl, "ei%s1" % sl, "d1%s0" % sl, "d1%s1" % sl, "c0" + sl, "th0" + sl, "th1" + sl])
                last = parents(t, slot, [gate2])
        for i, (t, slot) in enumerate(sorted(made, key=lambda x: x[1] < 2)):
            plain(t, slot, i % 2, [last])
    for p in range(2):
        dma("y", T.yj[:, 256 * p:256 * p + 256], T.jf[:, 0:2, p, :], ["jf0", "jf1"], (), "fin", 262144)

    def finish_out(land, sem, c0, n, engs):
        runs = []
        for k in range(4):
            if k == kme:
                continue
            ch = topo.chip(cores[CHAIN[k]])
            if runs and runs[-1][1] == k and runs[-1][2] == ch:
                runs[-1][1] = k + 1
            else:
                runs.append([k, k + 1, ch])
            arrive(sem + str(k), CHAIN[k], [sem + str(k)])
        for k0, k1, _ in runs:
            for q in range(4):
                dma(engs, T.ytau[32 * k0:32 * k1, 512 * q + c0:512 * q + c0 + n], land[k0:k1, 32 * q:32 * q + 32, :],
                    [sem + str(k) for k in range(k0, k1)], (), "fin", 800 * n)

    if lister:
        finish_out(T.dout, "oa", 0, 512, "ys")
        return ops

    dma("y", T.xl[:, xo(2 * rank + 1):xo(2 * rank + 1) + 1024], T.dx[kme], dxk, ["xl%d" % (2 * rank), "xl%d" % (2 * rank + 1)], "lxl", 300000)
    for r in range(1, nr):
        if r != rank:
            arrive("xa%d" % r, r, ["xl%d" % (2 * r), "xl%d" % (2 * r + 1)])
    first = len(topo.engines(relays(T, topo).get(kme, cores[0]), core))
    arrive("xa0", 0, ["xl0", "wb0"], first)
    arrive("tba", 0, ["xl1"], first)
    for t in range(2 * nr):
        frm = CONV[t][0] if t in CONV else t // 2
        arrive("ja%d" % t, frm, ["ju%d" % t], len(list_engines(cores[frm])[core]))
    b0 = xo(-1)
    for d in range(1, 4):
        p, c = 128 - 32 * d, b0 + 512 * d
        dma("y", T.xl[0:p, c:c + 512], T.xl[32 * d:128, b0:b0 + 512], ["wb0"], ["wb%da" % d], "lwb", 400000)
        dma("y", T.xl[p:128, c:c + 512], T.xl[0:32 * d, b0:b0 + 512], ["wb0"], ["wb%db" % d], "lwb", 400000)

    wins = [T.w0, T.w1]
    prevop = {}
    bank = {"30": 0, "10": 1, "11": 2, "12": 3, "33": 6, "13": 7}
    lo, hi = slice(0, 64), slice(64, 128)

    def wkeys(t):
        if t < 0:
            return ["wb0"] + ["wb%d%s" % (d, x) for d in range(1, 4) for x in "ab"]
        return ["w%d%s%d" % (t % 2, x, c) for x in ("0", "1", "2a", "2b", "3a", "3b") for c in range(4)]

    def xload(t):
        xb = 4 + t % 2
        prevop["p"] = op("p", 384 * PC + 20, lambda q, e: q.matmul(pb[xb][:, 0:384], T.ids[:, t, :], T.xl[:, xo(t) + 128:xo(t) + 512], True, True),
                         ["ids%d" % t, "xl%d" % t], ["pb%d" % xb, "xq%d" % t], after=[prevop["p"]] if "p" in prevop else [])

    def xscale(t, aft):
        c = T.xl[:, xo(t):xo(t) + 128]
        return copy("v", c, c, 128, ["xl%d" % t], ["xm%d" % t], scale=float(2 ** (t + 1)), vf=0.5, after=aft)

    def send_out(t, obk, land, sem, c0, n, engs):
        r = t // 2
        if r == rank:
            for q in range(4):
                dma(engs, T.ytau[32 * kme:32 * kme + 32, 512 * q + c0:512 * q + c0 + n], T.ob[32 * q:32 * q + 32, r, c0:c0 + n], obk, (), "fin", 512 * n)
            finish_out(land, sem, c0, n, engs)
        else:
            remote(r, land[kme], T.ob[:, r, c0:c0 + n], sem + str(kme), obk)

    def step(t):
        win = T.xl[:, b0:b0 + W] if t == 0 else wins[(t - 1) % 2][:, 0:W]
        wo, wk, z = wins[t % 2], wkeys(t - 1), t % 2
        final = t == 2 * nr - 1
        juk = "ju%d" % t

        def call(e, name):
            aft = [prevop[e]] if e in prevop else []
            if name == "x":
                return xscale(t + 1, aft)
            c = int(name[-1])
            a, b = 128 * c, 128 * c + 128
            ak, ok = "acc%d%d" % (z, c), "w%d0%d" % (z, c)
            j1, j2 = T.ju[:, t, 8 * c:8 * c + 8], T.ju[:, t, 32 + 8 * c:40 + 8 * c]
            acc = T.acc[:, z, a:b]
            if name[0] == "o":
                to = OUT_AT[t]
                return copy(e, T.ob[:, to // 2, 256 * c:256 * c + 256], wins[to % 2][:, 256 * c:256 * c + 256], 256,
                            ["w%d0%d" % (to % 2, i) for i in (2 * c, 2 * c + 1)], ["ob%d%d" % (to, c)], scale=2.0 ** -(to + 1), after=aft)
            if name[0] == "e":
                return copy(e, T.ob[:, t // 2, a:b], wo[:, a:b], 128, [ok], ["ob%d%d" % (t, c)], scale=2.0 ** -(t + 1), after=aft)
            if name[0] == "g":
                return op("s", gat(128), lambda q, e_: q.activation(acc, win.indirect(j2), AF.Copy), wk + [juk], [ak], after=aft)
            if name == "a0":
                return op("v", gat(128), lambda q, e_: q.tensor_tensor(acc, win.indirect(j2), T.xl[:, xo(t):xo(t) + 128], ALU.add),
                          wk + [juk, "xm%d" % t], [ak], after=aft)
            if name[0] == "a":
                xb = 4 + z
                return tt(acc, pb[xb][:, a - 128:b - 128], acc, ALU.add, 128, [ak, "xq%d" % t], [ak, "pb%d" % xb], after=aft)
            if name[0] == "b":
                return op("v", gat(128), lambda q, e_: q.tensor_tensor(wo[:, a:b], win.indirect(j1), acc, ALU.add), wk + [juk, ak], [ok], after=aft)
            d = int(name[1])
            o = 512 * d
            if name[0] == "p":
                bk = bank[name[1:]]
                return op("p", 512 * PC + 20, lambda q, e_: q.matmul(pb[bk][:, 0:128], T.rot[:, 32 * d:32 * d + 128], wo[:, a:b], True, True),
                          [ok, "rot"], ["pb%d" % bk, "tn%d" % bk], after=aft)
            if len(name) == 3:
                bk = bank[name[1:]]
                wr = ["w%d1%d" % (z, c)] if d == 1 else ["w%d3a%d" % (z, c), "w%d3b%d" % (z, c)]
                return copy(e, wo[:, o + a:o + b], pb[bk][:, 0:128], 128, ["tn%d" % bk], wr + ["pb%d" % bk], after=aft)
            to, frm = (lo, hi) if name[2] == "a" else (hi, lo)
            wr = ["w%d%d%s%d" % (z, d, name[2], c)]
            if d == 2:
                return copy(e, wo[to, o + a:o + b], wo[frm, a:b], 128, [ok], wr, after=aft)
            bk = bank["1%d" % c]
            return copy(e, wo[to, o + a:o + b], pb[bk][frm, 0:128], 128, ["tn%d" % bk], wr + ["pb%d" % bk], after=aft)

        pattern = STEP_LAST if final else STEP_O if t in OUT_AT else STEP
        if t < 2:
            pattern = [x for x in pattern if x != "v:x"] + ["v:x"]
        elif not final:
            xload(t + 1)
        for item in pattern:
            prevop[item[0]] = call(item[0], item[2:])
        if t < 2:
            xload(t + 1)
        if final:
            send_out(t, ["ob%d0" % t, "ob%d1" % t], T.dh0, "h0", 0, 256, "y")
            send_out(t, ["ob%d2" % t, "ob%d3" % t], T.dh1, "h1", 256, 256, "ys")
        elif t in OUT_AT:
            send_out(OUT_AT[t], ["ob%d%d" % (OUT_AT[t], c) for c in range(2)], T.dout, "oa", 0, 512, "y")

    base = len(ops)
    xload(0)
    prevop["v"] = xscale(0, [])
    for t in range(2 * nr):
        step(t)
    for o in ops[base:]:
        o["prio"] -= 10000
    return ops


def arrivals(T, topo):
    est = {}
    for _ in range(6):
        new = {}
        for core in T.cores:
            ops = plan(core, T, topo, est)
            order = schedule(ops)[0]
            busy = {True: 0.0, False: 0.0}
            for i in order["g"]:
                for to, sem, nbytes, way in ops[i].get("to", ()):
                    t0 = ops[i]["start"] + ops[i]["cost"]["g"]
                    if way in (True, False):
                        busy[way] = max(busy[way], t0) + nbytes / (200.0 if way else 80.0)
                    else:
                        busy[True] = max(busy[True], t0) + nbytes / 200.0
                        busy[way] = max(busy.get(way, 0.0), busy[True] + 2500.0) + nbytes / 80.0
                    new[(to, sem)] = max(new.get((to, sem), 0.0), busy[way] + 2000.0)
        est = new
    return est


def rank_program(g, core, T, topo):
    if T.rank_of(core) is None:
        for k, c in relays(T, topo).items():
            if c == core:
                relay_program(g, core, k, T, topo)
        return
    if "est" not in PLANS:
        PLANS["est"] = arrivals(T, topo)
    ops = plan(core, T, topo, PLANS["est"])
    order, eng, _ = schedule(ops)
    emit(g, T, ops, order, eng)
